import numpy as np, ml_dtypes
CORES = [88,96,104,112,120,216,224,232,240,248]
N = 10
QP = 64
WID = [32,32,16,32,64,64,48,16,48,64]
def setup_inputs(rng):
    return {"q": rng.standard_normal((N, 128, QP), dtype=np.float32).astype(ml_dtypes.bfloat16), "k": rng.standard_normal((N, 128, 128), dtype=np.float32).astype(ml_dtypes.bfloat16), "v": rng.standard_normal((N, 128, 128), dtype=np.float32).astype(ml_dtypes.bfloat16)}
def setup_inputs_big(rng):
    d = setup_inputs(rng)
    for k in ("q", "k", "v"): d[k] = (d[k].astype(np.float32) * 1024.0).astype(d[k].dtype)
    return d
def setup_inputs_small(rng):
    d = setup_inputs(rng)
    for k in ("q", "k", "v"): d[k] = (d[k].astype(np.float32) * (1 / 1024.0)).astype(d[k].dtype)
    return d
def setup_inputs_apart(rng):
    d = setup_inputs(rng)
    f = (10.0 ** rng.permutation(np.linspace(-1.5, 1.5, N))).astype(np.float32).reshape(N, 1, 1)
    for k in ("q", "k", "v"): d[k] = (d[k].astype(np.float32) * f).astype(d[k].dtype)
    return d
def whole(q, k, v):
    Q, K, V = q.astype(np.float64), k.astype(np.float64), v.astype(np.float64)
    y = np.zeros((N, 128, QP))
    for r in range(N):
        S = [K[j].T @ Q[r] for j in range(N)]
        m = np.max([s.max(axis=0) for s in S], axis=0)
        y[r] = sum(V[j].T @ np.maximum(S[j] - 0.5 * m, 0.0) for j in range(N))
    return {"y": y.astype(ml_dtypes.bfloat16)}
def reference(q, k, v):
    o = whole(q, k, v)["y"].copy()
    for r in range(N):
        o[r][:, WID[r]:] = np.nan
    return {"y": o}

@@ -1,0 +1,263 @@
+from concourse.bass import DstId, RemoteDMATransfer
+from concourse.mybir import AluOpType
+
+NCORES = 256
+N = 10
+KW = 128
+SLOT = 2 * KW
+NDIRECT = 3
+NBANK = N // 2
+
+SCRATCH = {
+    "kvd": ("dram", [128, SLOT], "bfloat16"),
+    "idd": ("dram", [65, 64], "bfloat16"),
+    "kv": ("sbuf", [128, N * SLOT], "bfloat16"),
+    "qs": ("sbuf", [128, 64], "bfloat16"),
+    "zi": ("sbuf", [128, 65], "bfloat16"),
+    "ident": ("sbuf", [128, 64], "bfloat16"),
+    "nh": ("sbuf", [128, KW], "bfloat16"),
+    "zeros": ("sbuf", [128, 128], "float32"),
+    "ra": ("sbuf", [128, 64], "float32"),
+    "rb": ("sbuf", [128, 64], "float32"),
+    "tr": ("sbuf", [128, 64], "float32"),
+    "mcol": ("sbuf", [128, 8], "bfloat16"),
+    "mrow": ("sbuf", [128, 64], "bfloat16"),
+    "p": ("sbuf", [128, N * 64], "bfloat16"),
+    "ysb": ("sbuf", [128, 64], "bfloat16"),
+    "pa0": ("psum", [128, 512], "float32"),
+    "pa1": ("psum", [128, 512], "float32"),
+    "ps0": ("psum", [128, 512], "float32"),
+    "ps1": ("psum", [128, 512], "float32"),
+    "ps2": ("psum", [128, 512], "float32"),
+    "ps3": ("psum", [128, 512], "float32"),
+    "ps4": ("psum", [128, 512], "float32"),
+    "py": ("psum", [128, 512], "float32"),
+}
+SEMAPHORES = ["ldd", "lds", "hin", "sent", "ms", "mz", "id1", "id2", "st", "mx", "tr", "tp", "mr", "sb", "rl", "yd",
+              "yc", "stored"] + ["arr%d" % j for j in range(N)]
+
+_CACHE = {}
+
+
+def _combos(items, k):
+    if k == 0:
+        return [[]]
+    out = []
+    for i in range(len(items) - k + 1):
+        for rest in _combos(items[i + 1:], k - 1):
+            out.append([items[i]] + rest)
+    return out
+
+
+def _plan(T, topo):
+    if "plan" in _CACHE:
+        return _CACHE["plan"]
+    cores = list(T.cores)
+
+    def where(c):
+        return (topo.host(c), topo.chip(c))
+
+    mate_of = {}
+
+    def mate_chip(c):
+        if where(c) not in mate_of:
+            mate_of[where(c)] = [where(m) for m in range(NCORES) if topo.mates(c, m)][0]
+        return mate_of[where(c)]
+
+    def links(x, d):
+        if where(x) == where(d):
+            return []
+        die = topo.die(x)
+        if topo.same_plane(x, d):
+            return [("out", where(x), die), ("in", where(d), die)]
+        way = [("mate", where(x), die)]
+        if not topo.mates(x, d):
+            way += [("out", mate_chip(x), die), ("in", where(d), die)]
+        return way
+
+    options = {}
+    for j in range(N):
+        c0 = cores[j]
+        others = [r for r in range(N) if r != j]
+        same = [r for r in others if topo.may_write(c0, cores[r])]
+        owners = [c for c in range(NCORES) if where(c) == where(c0) and c != c0
+                  and all(topo.may_write(c, cores[r]) for r in others)]
+        far = [c for c in owners if topo.die(c) != topo.die(c0)]
+        near = [c for c in owners if topo.die(c) == topo.die(c0)]
+        options[j] = []
+        for direct in _combos(same, NDIRECT):
+            rest = [r for r in others if r not in direct]
+            for f in _combos(rest, 4):
+                nr = [r for r in rest if r not in f]
+                opt = [(c0, direct), (far[0], f[:2]), (far[1], f[2:]), (near[0], nr[:1]), (near[1], nr[1:])]
+                use = []
+                for x, ds in opt:
+                    for r in ds:
+                        use += links(x, cores[r])
+                options[j].append((opt, use))
+
+    def cost(pick):
+        load = {}
+        for j in range(N):
+            for l in options[j][pick[j]][1]:
+                load[l] = load.get(l, 0) + 1
+        return sum(v ** 3 for v in load.values())
+
+    pick = [0] * N
+    best = cost(pick)
+    changed = True
+    while changed:
+        changed = False
+        for j in range(N):
+            for o in range(len(options[j])):
+                trial = pick[:j] + [o] + pick[j + 1:]
+                c = cost(trial)
+                if c < best:
+                    best, pick, changed = c, trial, True
+
+    carry = {j: options[j][pick[j]][0] for j in range(N)}
+    helper = {}
+    due = {r: [(-1.0, r)] for r in range(N)}
+    for j in range(N):
+        for pos, (x, ds) in enumerate(carry[j]):
+            if pos > 0:
+                helper[x] = (j, ds)
+            for n, r in enumerate(ds):
+                due[r].append(((n if pos == 0 else 2.0 + n + 0.25 * pos), j))
+    order = {r: [j for _, j in sorted(due[r])] for r in range(N)}
+    _CACHE["plan"] = (carry, helper, order)
+    return _CACHE["plan"]
+
+
+def _send(g, T, topo, core, dst_cores, src, dst, rsem):
+    mask = topo.mask(core, dst_cores[0])
+    ids = []
+    for d in dst_cores:
+        mask &= topo.mask(core, d)
+        rid, pid = topo.addr(d, core)
+        ids.append(DstId(rid=rid, pnc=pid))
+    g.remote_dma_fused([RemoteDMATransfer(dst_ids=ids, dma_engine_mask=mask, remote_sem=rsem, srcs=[src],
+                                          dsts=[dst] * len(ids), alu_op=0)], local_sem=T.sem.sent)
+    return bin(mask).count("1")
+
+
+def rank_program(g, core, T, topo):
+    carry, helper, order = _plan(T, topo)
+    cores = list(T.cores)
+    sem = T.sem
+    rank = T.rank_of(core)
+
+    if rank is None:
+        if core not in helper:
+            return
+        j, dests = helper[core]
+        c0 = cores[j]
+        g.wait_ge(sem.hin, bin(topo.mask(c0, core)).count("1"))
+        n = _send(g, T, topo, core, [cores[r] for r in dests], T.kvd[:], T.kv[:, j * SLOT:(j + 1) * SLOT],
+                  sem["arr%d" % j])
+        g.wait_ge(sem.sent, n)
+        return
+
+    W = T.tables["WID"][rank]
+    te, ve, sy, sc = g.tensor, g.vector, g.sync, g.scalar
+    own = rank * SLOT
+
+    def kslot(j):
+        return T.kv[:, j * SLOT:j * SLOT + KW]
+
+    def vslot(j):
+        return T.kv[:, j * SLOT + KW:(j + 1) * SLOT]
+
+    sy.dma_start(T.kvd[:, 0:KW], T.k[:]).then_inc(sem.ldd, 16)
+    sc.dma_start(T.kvd[:, KW:SLOT], T.v[:]).then_inc(sem.ldd, 16)
+    sy.dma_start(kslot(rank), T.k[:]).then_inc(sem.lds, 16)
+    sc.dma_start(vslot(rank), T.v[:]).then_inc(sem.lds, 16)
+    sy.dma_start(T.qs[:], T.q[:]).then_inc(sem.lds, 16)
+
+    g.wait_ge(sem.ldd, 32)
+    sent = _send(g, T, topo, core, [x for x, _ in carry[rank][1:]], T.kvd[:], T.kvd[:], sem.hin)
+    sent += _send(g, T, topo, core, [cores[r] for r in carry[rank][0][1]], T.kvd[:], T.kv[:, own:own + SLOT],
+                  sem["arr%d" % rank])
+
+    ve.memset(T.zi[0:64, 1:65], 0.0).then_inc(sem.ms, 1)
+    ve.memset(T.zi[0:64, 0:1], 1.0).then_inc(sem.ms, 1)
+    ve.memset(T.nh[0:1, :], -0.5).then_inc(sem.mz, 1)
+    ve.memset(T.zeros[:, 0:2 * W], 0.0).then_inc(sem.mz, 1)
+    ps = [T["ps%d" % b] for b in range(NBANK)]
+    pa = [T.pa0, T.pa1]
+    for b in range(NBANK):
+        ve.memset(ps[b][:, W:2 * W], 0.0).then_inc(sem.mz, 1)
+    nmz = 2 + NBANK
+    sc.wait_ge(sem.ms, 2)
+    sc.dma_start(T.idd[:], T.zi[0:64, :]).then_inc(sem.id1, 16)
+    sc.wait_ge(sem.id1, 16)
+    sc.dma_start(T.ident[0:64, :], T.idd[0:64, :]).then_inc(sem.id2, 16)
+
+    arrive = {}
+    for j in range(N):
+        for x, ds in carry[j]:
+            for r in ds:
+                if r == rank:
+                    m = topo.mask(x, core)
+                    for r2 in ds:
+                        m &= topo.mask(x, cores[r2])
+                    arrive[j] = bin(m).count("1")
+    q = T.qs[:, 0:W]
+    te.wait_ge(sem.lds, 48)
+    te.wait_ge(sem.mz, nmz)
+    ve.wait_ge(sem.mz, nmz)
+    for i, j in enumerate(order[rank]):
+        if j != rank:
+            te.wait_ge(sem["arr%d" % j], arrive[j])
+        if i >= 2:
+            te.wait_ge(sem.mx, 2 * (i - 1))
+        bank = pa[i % 2]
+        te.matmul(bank[0:W, 0:KW], q, kslot(j), True, True).then_inc(sem.st, 1)
+        te.matmul(ps[i // 2][:, (i % 2) * W:(i % 2 + 1) * W], kslot(j), q, i % 2 == 0, False)
+        ve.wait_ge(sem.st, i + 1)
+        if i == 0:
+            ve.tensor_copy(T.ra[0:W, :], bank[0:W, 0:64]).then_inc(sem.mx, 1)
+        else:
+            ve.wait_ge(sem.mx, 2 * i)
+            ve.tensor_tensor(T.ra[0:W, :], bank[0:W, 0:64], T.rb[0:W, :], AluOpType.max).then_inc(sem.mx, 1)
+        ve.wait_ge(sem.mx, 2 * i + 1)
+        ve.tensor_tensor(T.rb[0:W, :], bank[0:W, 64:128], T.ra[0:W, :], AluOpType.max).then_inc(sem.mx, 1)
+
+    ve.wait_ge(sem.mx, 2 * N)
+    src, lo, width, step = T.rb, 0, 32, 0
+    while width >= 1:
+        if width > 1:
+            out = T.tr[0:W, 64 - 2 * width:64 - width]
+        else:
+            out = T.mcol[0:W, 0:1]
+        ve.tensor_tensor(out, src[0:W, lo:lo + width], src[0:W, lo + width:lo + 2 * width],
+                         AluOpType.max).then_inc(sem.tr, 1)
+        step += 1
+        if width > 1:
+            ve.wait_ge(sem.tr, step)
+        src, lo, width = T.tr, 64 - 2 * width, width // 2
+    te.wait_ge(sem.tr, step)
+    te.wait_ge(sem.id2, 16)
+    te.matmul(T.py[0:1, 0:W], T.mcol[0:W, 0:1], T.ident[0:W, 0:W], True, True).then_inc(sem.tp, 1)
+    ve.wait_ge(sem.tp, 1)
+    ve.tensor_copy(T.mrow[0:1, 0:W], T.py[0:1, 0:W]).then_inc(sem.mr, 1)
+
+    te.wait_ge(sem.mr, 1)
+    for b in range(NBANK):
+        te.matmul(ps[b][:, 0:W], T.nh[0:1, :], T.mrow[0:1, 0:W], False, False).then_inc(sem.sb, 1)
+        te.matmul(ps[b][:, W:2 * W], T.nh[0:1, :], T.mrow[0:1, 0:W], False, True).then_inc(sem.sb, 1)
+        ve.wait_ge(sem.sb, 2 * (b + 1))
+        ve.tensor_tensor(T.p[:, 2 * b * W:2 * (b + 1) * W], ps[b][:, 0:2 * W], T.zeros[:, 0:2 * W],
+                         AluOpType.max).then_inc(sem.rl, 1)
+    for i, j in enumerate(order[rank]):
+        if i % 2 == 0:
+            te.wait_ge(sem.rl, i // 2 + 1)
+        mm = te.matmul(T.py[:, 0:W], vslot(j), T.p[:, i * W:(i + 1) * W], i == 0, i == N - 1)
+        if i == N - 1:
+            mm.then_inc(sem.yd, 1)
+    ve.wait_ge(sem.yd, 1)
+    ve.tensor_copy(T.ysb[:, 0:W], T.py[:, 0:W]).then_inc(sem.yc, 1)
+    sy.wait_ge(sem.yc, 1)
+    sy.dma_start(T.y[:, 0:W], T.ysb[:, 0:W]).then_inc(sem.stored, 16)
+    sy.wait_ge(sem.stored, 16)
+    g.wait_ge(sem.sent, sent)

@@ -1,27 +1,23 @@
 from concourse.bass import DstId, RemoteDMATransfer
-from concourse.mybir import AluOpType
+from concourse.mybir import AluOpType, AxisListType
 
 NCORES = 256
 N = 10
 KW = 128
-SLOT = 2 * KW
 NDIRECT = 3
 NBANK = N // 2
 
 SCRATCH = {
-    "kvd": ("dram", [128, SLOT], "bfloat16"),
-    "idd": ("dram", [65, 64], "bfloat16"),
-    "kv": ("sbuf", [128, N * SLOT], "bfloat16"),
+    "kd": ("dram", [128, KW], "bfloat16"),
+    "vd": ("dram", [128, KW], "bfloat16"),
+    "kk": ("sbuf", [128, N * KW], "bfloat16"),
+    "vv": ("sbuf", [128, N * KW], "bfloat16"),
     "qs": ("sbuf", [128, 64], "bfloat16"),
-    "zi": ("sbuf", [128, 65], "bfloat16"),
-    "ident": ("sbuf", [128, 64], "bfloat16"),
-    "nh": ("sbuf", [128, KW], "bfloat16"),
-    "zeros": ("sbuf", [128, 128], "float32"),
-    "ra": ("sbuf", [128, 64], "float32"),
-    "rb": ("sbuf", [128, 64], "float32"),
-    "tr": ("sbuf", [128, 64], "float32"),
-    "mcol": ("sbuf", [128, 8], "bfloat16"),
-    "mrow": ("sbuf", [128, 64], "bfloat16"),
+    "ones": ("sbuf", [128, KW], "bfloat16"),
+    "id2": ("sbuf", [128, KW], "bfloat16"),
+    "dd": ("sbuf", [128, KW], "bfloat16"),
+    "mc": ("sbuf", [128, 16], "float32"),
+    "mm": ("sbuf", [128, 4], "float32"),
     "p": ("sbuf", [128, N * 64], "bfloat16"),
     "ysb": ("sbuf", [128, 64], "bfloat16"),
     "pa0": ("psum", [128, 512], "float32"),
@@ -33,8 +29,8 @@ SCRATCH = {
     "ps4": ("psum", [128, 512], "float32"),
     "py": ("psum", [128, 512], "float32"),
 }
-SEMAPHORES = ["ldd", "lds", "hin", "sent", "ms", "mz", "id1", "id2", "st", "mx", "tr", "tp", "mr", "sb", "rl", "yd",
-              "yc", "stored"] + ["arr%d" % j for j in range(N)]
+SEMAPHORES = (["ldk", "ldv", "lds", "lsv", "hk", "hv", "sent", "on", "mz", "idn", "st", "mx", "tr", "dr", "sb", "rl", "yd",
+               "yc", "stored"] + ["ka%d" % j for j in range(N)] + ["va%d" % j for j in range(N)])
 
 _CACHE = {}
 
@@ -147,51 +143,51 @@ def rank_program(g, core, T, topo):
     sem = T.sem
     rank = T.rank_of(core)
 
+    def kslot(j):
+        return T.kk[:, j * KW:(j + 1) * KW]
+
+    def vslot(j):
+        return T.vv[:, j * KW:(j + 1) * KW]
+
     if rank is None:
         if core not in helper:
             return
         j, dests = helper[core]
-        c0 = cores[j]
-        g.wait_ge(sem.hin, bin(topo.mask(c0, core)).count("1"))
-        n = _send(g, T, topo, core, [cores[r] for r in dests], T.kvd[:], T.kv[:, j * SLOT:(j + 1) * SLOT],
-                  sem["arr%d" % j])
+        landed = bin(topo.mask(cores[j], core)).count("1")
+        g.wait_ge(sem.hk, landed)
+        n = _send(g, T, topo, core, [cores[r] for r in dests], T.kd[:], kslot(j), sem["ka%d" % j])
+        g.wait_ge(sem.hv, landed)
+        n += _send(g, T, topo, core, [cores[r] for r in dests], T.vd[:], vslot(j), sem["va%d" % j])
         g.wait_ge(sem.sent, n)
         return
 
     W = T.tables["WID"][rank]
     te, ve, sy, sc = g.tensor, g.vector, g.sync, g.scalar
-    own = rank * SLOT
 
-    def kslot(j):
-        return T.kv[:, j * SLOT:j * SLOT + KW]
-
-    def vslot(j):
-        return T.kv[:, j * SLOT + KW:(j + 1) * SLOT]
-
-    sy.dma_start(T.kvd[:, 0:KW], T.k[:]).then_inc(sem.ldd, 16)
-    sc.dma_start(T.kvd[:, KW:SLOT], T.v[:]).then_inc(sem.ldd, 16)
+    sy.dma_start(T.kd[:], T.k[:]).then_inc(sem.ldk, 16)
+    sc.dma_start(T.vd[:], T.v[:]).then_inc(sem.ldv, 16)
     sy.dma_start(kslot(rank), T.k[:]).then_inc(sem.lds, 16)
-    sc.dma_start(vslot(rank), T.v[:]).then_inc(sem.lds, 16)
-    sy.dma_start(T.qs[:], T.q[:]).then_inc(sem.lds, 16)
+    sc.dma_start(T.qs[:], T.q[:]).then_inc(sem.lds, 16)
+    sc.dma_start(vslot(rank), T.v[:]).then_inc(sem.lsv, 16)
 
-    g.wait_ge(sem.ldd, 32)
-    sent = _send(g, T, topo, core, [x for x, _ in carry[rank][1:]], T.kvd[:], T.kvd[:], sem.hin)
-    sent += _send(g, T, topo, core, [cores[r] for r in carry[rank][0][1]], T.kvd[:], T.kv[:, own:own + SLOT],
-                  sem["arr%d" % rank])
+    carriers = [x for x, _ in carry[rank][1:]]
+    direct = [cores[r] for r in carry[rank][0][1]]
+    g.wait_ge(sem.ldk, 16)
+    sent = _send(g, T, topo, core, carriers, T.kd[:], T.kd[:], sem.hk)
+    sent += _send(g, T, topo, core, direct, T.kd[:], kslot(rank), sem["ka%d" % rank])
+    g.wait_ge(sem.ldv, 16)
+    sent += _send(g, T, topo, core, carriers, T.vd[:], T.vd[:], sem.hv)
+    sent += _send(g, T, topo, core, direct, T.vd[:], vslot(rank), sem["va%d" % rank])
 
-    ve.memset(T.zi[0:64, 1:65], 0.0).then_inc(sem.ms, 1)
-    ve.memset(T.zi[0:64, 0:1], 1.0).then_inc(sem.ms, 1)
-    ve.memset(T.nh[0:1, :], -0.5).then_inc(sem.mz, 1)
-    ve.memset(T.zeros[:, 0:2 * W], 0.0).then_inc(sem.mz, 1)
+    ve.memset(T.ones[:], 1.0).then_inc(sem.on, 1)
     ps = [T["ps%d" % b] for b in range(NBANK)]
     pa = [T.pa0, T.pa1]
     for b in range(NBANK):
         ve.memset(ps[b][:, W:2 * W], 0.0).then_inc(sem.mz, 1)
-    nmz = 2 + NBANK
-    sc.wait_ge(sem.ms, 2)
-    sc.dma_start(T.idd[:], T.zi[0:64, :]).then_inc(sem.id1, 16)
-    sc.wait_ge(sem.id1, 16)
-    sc.dma_start(T.ident[0:64, :], T.idd[0:64, :]).then_inc(sem.id2, 16)
+    g.wait_ge(sem.on, 1)
+    for h in range(2):
+        g.affine_select(T.id2[0:W, h * W:(h + 1) * W], T.ones[0:W, h * W:(h + 1) * W], [[-1, W]], AluOpType.is_equal, 0.0,
+                        0, 1).then_inc(sem.idn, 1)
 
     arrive = {}
     for j in range(N):
@@ -203,55 +199,41 @@ def rank_program(g, core, T, topo):
                         m &= topo.mask(x, cores[r2])
                     arrive[j] = bin(m).count("1")
     q = T.qs[:, 0:W]
-    te.wait_ge(sem.lds, 48)
-    te.wait_ge(sem.mz, nmz)
-    ve.wait_ge(sem.mz, nmz)
+    te.wait_ge(sem.lds, 32)
+    te.wait_ge(sem.mz, NBANK)
     for i, j in enumerate(order[rank]):
         if j != rank:
-            te.wait_ge(sem["arr%d" % j], arrive[j])
+            te.wait_ge(sem["ka%d" % j], arrive[j])
         if i >= 2:
-            te.wait_ge(sem.mx, 2 * (i - 1))
+            te.wait_ge(sem.mx, i - 1)
         bank = pa[i % 2]
         te.matmul(bank[0:W, 0:KW], q, kslot(j), True, True).then_inc(sem.st, 1)
         te.matmul(ps[i // 2][:, (i % 2) * W:(i % 2 + 1) * W], kslot(j), q, i % 2 == 0, False)
         ve.wait_ge(sem.st, i + 1)
-        if i == 0:
-            ve.tensor_copy(T.ra[0:W, :], bank[0:W, 0:64]).then_inc(sem.mx, 1)
-        else:
-            ve.wait_ge(sem.mx, 2 * i)
-            ve.tensor_tensor(T.ra[0:W, :], bank[0:W, 0:64], T.rb[0:W, :], AluOpType.max).then_inc(sem.mx, 1)
-        ve.wait_ge(sem.mx, 2 * i + 1)
-        ve.tensor_tensor(T.rb[0:W, :], bank[0:W, 64:128], T.ra[0:W, :], AluOpType.max).then_inc(sem.mx, 1)
+        ve.tensor_reduce(T.mc[0:W, i:i + 1], bank[0:W, 0:KW], AxisListType.X, AluOpType.max).then_inc(sem.mx, 1)
 
-    ve.wait_ge(sem.mx, 2 * N)
-    src, lo, width, step = T.rb, 0, 32, 0
-    while width >= 1:
-        if width > 1:
-            out = T.tr[0:W, 64 - 2 * width:64 - width]
-        else:
-            out = T.mcol[0:W, 0:1]
-        ve.tensor_tensor(out, src[0:W, lo:lo + width], src[0:W, lo + width:lo + 2 * width],
-                         AluOpType.max).then_inc(sem.tr, 1)
-        step += 1
-        if width > 1:
-            ve.wait_ge(sem.tr, step)
-        src, lo, width = T.tr, 64 - 2 * width, width // 2
-    te.wait_ge(sem.tr, step)
-    te.wait_ge(sem.id2, 16)
-    te.matmul(T.py[0:1, 0:W], T.mcol[0:W, 0:1], T.ident[0:W, 0:W], True, True).then_inc(sem.tp, 1)
-    ve.wait_ge(sem.tp, 1)
-    ve.tensor_copy(T.mrow[0:1, 0:W], T.py[0:1, 0:W]).then_inc(sem.mr, 1)
+    ve.wait_ge(sem.mx, N)
+    ve.tensor_reduce(T.mm[0:W, 0:1], T.mc[0:W, 0:N], AxisListType.X, AluOpType.max).then_inc(sem.tr, 1)
+    ve.wait_ge(sem.tr, 1)
+    ve.wait_ge(sem.idn, 2)
+    ve.tensor_scalar(T.dd[0:W, 0:2 * W], T.id2[0:W, 0:2 * W], T.mm[0:W, 0:1], -0.5, AluOpType.mult,
+                     AluOpType.mult).then_inc(sem.dr, 1)
 
-    te.wait_ge(sem.mr, 1)
+    te.wait_ge(sem.dr, 1)
+    te.wait_ge(sem.on, 1)
     for b in range(NBANK):
-        te.matmul(ps[b][:, 0:W], T.nh[0:1, :], T.mrow[0:1, 0:W], False, False).then_inc(sem.sb, 1)
-        te.matmul(ps[b][:, W:2 * W], T.nh[0:1, :], T.mrow[0:1, 0:W], False, True).then_inc(sem.sb, 1)
-        ve.wait_ge(sem.sb, 2 * (b + 1))
-        ve.tensor_tensor(T.p[:, 2 * b * W:2 * (b + 1) * W], ps[b][:, 0:2 * W], T.zeros[:, 0:2 * W],
+        te.matmul(ps[b][:, 0:2 * W], T.ones[0:W, :], T.dd[0:W, 0:2 * W], False, True).then_inc(sem.sb, 1)
+        ve.wait_ge(sem.sb, b + 1)
+        ve.tensor_scalar(T.p[:, 2 * b * W:2 * (b + 1) * W], ps[b][:, 0:2 * W], 0.0, None,
                          AluOpType.max).then_inc(sem.rl, 1)
+
     for i, j in enumerate(order[rank]):
         if i % 2 == 0:
             te.wait_ge(sem.rl, i // 2 + 1)
+        if j == rank:
+            te.wait_ge(sem.lsv, 16)
+        else:
+            te.wait_ge(sem["va%d" % j], arrive[j])
         mm = te.matmul(T.py[:, 0:W], vslot(j), T.p[:, i * W:(i + 1) * W], i == 0, i == N - 1)
         if i == N - 1:
             mm.then_inc(sem.yd, 1)

@@ -6,6 +6,7 @@ N = 10
 KW = 128
 NDIRECT = 3
 NBANK = N // 2
+LATE = 5
 
 SCRATCH = {
     "kd": ("dram", [128, KW], "bfloat16"),
@@ -13,9 +14,10 @@ SCRATCH = {
     "kk": ("sbuf", [128, N * KW], "bfloat16"),
     "vv": ("sbuf", [128, N * KW], "bfloat16"),
     "qs": ("sbuf", [128, 64], "bfloat16"),
-    "ones": ("sbuf", [128, KW], "bfloat16"),
-    "id2": ("sbuf", [128, KW], "bfloat16"),
-    "dd": ("sbuf", [128, KW], "bfloat16"),
+    "half": ("sbuf", [128, KW], "bfloat16"),
+    "idh": ("sbuf", [128, KW], "bfloat16"),
+    "zz": ("sbuf", [128, 2 * KW], "float32"),
+    "mb": ("sbuf", [128, 2 * KW], "bfloat16"),
     "mc": ("sbuf", [128, 16], "float32"),
     "mm": ("sbuf", [128, 4], "float32"),
     "p": ("sbuf", [128, N * 64], "bfloat16"),
@@ -29,8 +31,8 @@ SCRATCH = {
     "ps4": ("psum", [128, 512], "float32"),
     "py": ("psum", [128, 512], "float32"),
 }
-SEMAPHORES = (["ldk", "ldv", "lds", "lsv", "hk", "hv", "sent", "on", "mz", "idn", "st", "mx", "tr", "dr", "sb", "rl", "yd",
-               "yc", "stored"] + ["ka%d" % j for j in range(N)] + ["va%d" % j for j in range(N)])
+SEMAPHORES = (["ldk", "ldv", "lds", "lsv", "hk", "hv", "sent", "on", "mz", "idn", "fl", "st", "mx", "tr", "dr", "sb", "rl",
+               "yd", "yc", "stored"] + ["ka%d" % j for j in range(N)] + ["va%d" % j for j in range(N)])
 
 _CACHE = {}
 
@@ -179,14 +181,16 @@ def rank_program(g, core, T, topo):
     sent += _send(g, T, topo, core, carriers, T.vd[:], T.vd[:], sem.hv)
     sent += _send(g, T, topo, core, direct, T.vd[:], vslot(rank), sem["va%d" % rank])
 
-    ve.memset(T.ones[:], 1.0).then_inc(sem.on, 1)
+    ve.memset(T.half[:], -0.5).then_inc(sem.on, 1)
+    ve.memset(T.zz[:], 0.0).then_inc(sem.on, 1)
     ps = [T["ps%d" % b] for b in range(NBANK)]
-    pa = [T.pa0, T.pa1]
+    pa = [T.pa0, T.pa1, T.py]
+    NA = len(pa)
     for b in range(NBANK):
         ve.memset(ps[b][:, W:2 * W], 0.0).then_inc(sem.mz, 1)
-    g.wait_ge(sem.on, 1)
+    g.wait_ge(sem.on, 2)
     for h in range(2):
-        g.affine_select(T.id2[0:W, h * W:(h + 1) * W], T.ones[0:W, h * W:(h + 1) * W], [[-1, W]], AluOpType.is_equal, 0.0,
+        g.affine_select(T.idh[0:W, h * W:(h + 1) * W], T.half[0:W, h * W:(h + 1) * W], [[-1, W]], AluOpType.is_equal, 0.0,
                         0, 1).then_inc(sem.idn, 1)
 
     arrive = {}
@@ -199,30 +203,42 @@ def rank_program(g, core, T, topo):
                         m &= topo.mask(x, cores[r2])
                     arrive[j] = bin(m).count("1")
     q = T.qs[:, 0:W]
+
+    def scores(i, j):
+        te.matmul(ps[i // 2][:, (i % 2) * W:(i % 2 + 1) * W], kslot(j), q, i % 2 == 0, False)
+
     te.wait_ge(sem.lds, 32)
     te.wait_ge(sem.mz, NBANK)
+    te.matmul(pa[(N - 1) % NA][0:W, KW:2 * KW], q, kslot(rank), True, True).then_inc(sem.fl, 1)
+    ve.wait_ge(sem.on, 2)
+    ve.wait_ge(sem.fl, 1)
     for i, j in enumerate(order[rank]):
         if j != rank:
             te.wait_ge(sem["ka%d" % j], arrive[j])
-        if i >= 2:
-            te.wait_ge(sem.mx, i - 1)
-        bank = pa[i % 2]
+        if i >= NA:
+            te.wait_ge(sem.mx, i - NA + 1)
+        bank = pa[i % NA]
         te.matmul(bank[0:W, 0:KW], q, kslot(j), True, True).then_inc(sem.st, 1)
-        te.matmul(ps[i // 2][:, (i % 2) * W:(i % 2 + 1) * W], kslot(j), q, i % 2 == 0, False)
+        if i < N - LATE:
+            scores(i, j)
         ve.wait_ge(sem.st, i + 1)
-        ve.tensor_reduce(T.mc[0:W, i:i + 1], bank[0:W, 0:KW], AxisListType.X, AluOpType.max).then_inc(sem.mx, 1)
-
-    ve.wait_ge(sem.mx, N)
-    ve.tensor_reduce(T.mm[0:W, 0:1], T.mc[0:W, 0:N], AxisListType.X, AluOpType.max).then_inc(sem.tr, 1)
-    ve.wait_ge(sem.tr, 1)
-    ve.wait_ge(sem.idn, 2)
-    ve.tensor_scalar(T.dd[0:W, 0:2 * W], T.id2[0:W, 0:2 * W], T.mm[0:W, 0:1], -0.5, AluOpType.mult,
-                     AluOpType.mult).then_inc(sem.dr, 1)
+        if i < N - 1:
+            ve.tensor_reduce(T.mc[0:W, i:i + 1], bank[0:W, 0:KW], AxisListType.X, AluOpType.max).then_inc(sem.mx, 1)
+        if i == N - 2:
+            ve.wait_ge(sem.mx, N - 1)
+            ve.tensor_reduce(T.mm[0:W, 0:1], T.mc[0:W, 0:N - 1], AxisListType.X, AluOpType.max).then_inc(sem.tr, 1)
+        if i == N - 1:
+            ve.wait_ge(sem.tr, 1)
+            ve.tensor_tensor_scan(T.mb[0:W, 0:2 * KW], bank[0:W, 0:2 * KW], T.zz[0:W, 0:2 * KW], T.mm[0:W, 0:1],
+                                  AluOpType.max, AluOpType.add).then_inc(sem.dr, 1)
+    for i, j in enumerate(order[rank]):
+        if i >= N - LATE:
+            scores(i, j)
 
     te.wait_ge(sem.dr, 1)
-    te.wait_ge(sem.on, 1)
+    te.wait_ge(sem.idn, 2)
     for b in range(NBANK):
-        te.matmul(ps[b][:, 0:2 * W], T.ones[0:W, :], T.dd[0:W, 0:2 * W], False, True).then_inc(sem.sb, 1)
+        te.matmul(ps[b][:, 0:2 * W], T.mb[0:W, KW:2 * KW], T.idh[0:W, 0:2 * W], False, True).then_inc(sem.sb, 1)
         ve.wait_ge(sem.sb, b + 1)
         ve.tensor_scalar(T.p[:, 2 * b * W:2 * (b + 1) * W], ps[b][:, 0:2 * W], 0.0, None,
                          AluOpType.max).then_inc(sem.rl, 1)

@@ -1,5 +1,5 @@
 from concourse.bass import DstId, RemoteDMATransfer
-from concourse.mybir import AluOpType, AxisListType
+from concourse.mybir import AluOpType, AxisListType, ActivationFunctionType
 
 NCORES = 256
 N = 10
@@ -7,6 +7,8 @@ KW = 128
 NDIRECT = 3
 NBANK = N // 2
 LATE = 5
+WSHORT = 32
+STARTS = 12
 
 SCRATCH = {
     "kd": ("dram", [128, KW], "bfloat16"),
@@ -31,8 +33,8 @@ SCRATCH = {
     "ps4": ("psum", [128, 512], "float32"),
     "py": ("psum", [128, 512], "float32"),
 }
-SEMAPHORES = (["ldk", "ldv", "lds", "lsv", "hk", "hv", "sent", "on", "mz", "idn", "fl", "st", "mx", "tr", "dr", "sb", "rl",
-               "yd", "yc", "stored"] + ["ka%d" % j for j in range(N)] + ["va%d" % j for j in range(N)])
+SEMAPHORES = (["ldk", "ldv", "lds", "lsv", "hk", "hv", "sent", "on", "mz", "idn", "ci", "cz", "fl", "st", "mx", "tr", "dr",
+               "sb", "rl", "rs", "yd", "yc", "stored"] + ["ka%d" % j for j in range(N)] + ["va%d" % j for j in range(N)])
 
 _CACHE = {}
 
@@ -51,6 +53,7 @@ def _plan(T, topo):
     if "plan" in _CACHE:
         return _CACHE["plan"]
     cores = list(T.cores)
+    wid = list(T.tables["WID"])
 
     def where(c):
         return (topo.host(c), topo.chip(c))
@@ -73,6 +76,12 @@ def _plan(T, topo):
             way += [("out", mate_chip(x), die), ("in", where(d), die)]
         return way
 
+    def wide_first(rs):
+        return sorted(rs, key=lambda r: (-wid[r], r))
+
+    def over(r):
+        return max(wid[r] - WSHORT, 0)
+
     options = {}
     for j in range(N):
         c0 = cores[j]
@@ -86,32 +95,40 @@ def _plan(T, topo):
         for direct in _combos(same, NDIRECT):
             rest = [r for r in others if r not in direct]
             for f in _combos(rest, 4):
-                nr = [r for r in rest if r not in f]
-                opt = [(c0, direct), (far[0], f[:2]), (far[1], f[2:]), (near[0], nr[:1]), (near[1], nr[1:])]
+                nr = wide_first([r for r in rest if r not in f])
+                d = wide_first(direct)
+                fs = wide_first(f)
+                opt = [(c0, d), (far[0], [fs[0], fs[2]]), (far[1], [fs[1], fs[3]]), (near[0], nr[:1]), (near[1], nr[1:])]
                 use = []
                 for x, ds in opt:
                     for r in ds:
                         use += links(x, cores[r])
-                options[j].append((opt, use))
+                late = 100 * (over(fs[2]) + over(fs[3])) + 10 * over(d[-1])
+                options[j].append((opt, use, late))
 
     def cost(pick):
         load = {}
         for j in range(N):
             for l in options[j][pick[j]][1]:
                 load[l] = load.get(l, 0) + 1
-        return sum(v ** 3 for v in load.values())
+        return sum(v ** 3 for v in load.values()) + sum(options[j][pick[j]][2] for j in range(N))
 
-    pick = [0] * N
-    best = cost(pick)
-    changed = True
-    while changed:
-        changed = False
-        for j in range(N):
-            for o in range(len(options[j])):
-                trial = pick[:j] + [o] + pick[j + 1:]
-                c = cost(trial)
-                if c < best:
-                    best, pick, changed = c, trial, True
+    found = None
+    for s in range(STARTS):
+        pick = [(s * 7 + j * 3) % len(options[j]) if s else 0 for j in range(N)]
+        best = cost(pick)
+        changed = True
+        while changed:
+            changed = False
+            for j in range(N):
+                for o in range(len(options[j])):
+                    trial = pick[:j] + [o] + pick[j + 1:]
+                    c = cost(trial)
+                    if c < best:
+                        best, pick, changed = c, trial, True
+        if found is None or best < found[0]:
+            found = (best, pick)
+    pick = found[1]
 
     carry = {j: options[j][pick[j]][0] for j in range(N)}
     helper = {}
@@ -119,7 +136,7 @@ def _plan(T, topo):
     for j in range(N):
         for pos, (x, ds) in enumerate(carry[j]):
             if pos > 0:
-                helper[x] = (j, ds)
+                helper[x] = (j, ds, pos)
             for n, r in enumerate(ds):
                 due[r].append(((n if pos == 0 else 2.0 + n + 0.25 * pos), j))
     order = {r: [j for _, j in sorted(due[r])] for r in range(N)}
@@ -127,11 +144,17 @@ def _plan(T, topo):
     return _CACHE["plan"]
 
 
-def _send(g, T, topo, core, dst_cores, src, dst, rsem):
-    mask = topo.mask(core, dst_cores[0])
+def _mask(topo, core, reach):
+    mask = topo.mask(core, reach[0])
+    for d in reach:
+        mask &= topo.mask(core, d)
+    return mask
+
+
+def _send(g, T, topo, core, dst_cores, src, dst, rsem, reach=None):
+    mask = _mask(topo, core, list(dst_cores) + list(reach or []))
     ids = []
     for d in dst_cores:
-        mask &= topo.mask(core, d)
         rid, pid = topo.addr(d, core)
         ids.append(DstId(rid=rid, pnc=pid))
     g.remote_dma_fused([RemoteDMATransfer(dst_ids=ids, dma_engine_mask=mask, remote_sem=rsem, srcs=[src],
@@ -154,12 +177,27 @@ def rank_program(g, core, T, topo):
     if rank is None:
         if core not in helper:
             return
-        j, dests = helper[core]
-        landed = bin(topo.mask(cores[j], core)).count("1")
+        j, dests, pos = helper[core]
+        home = cores[j]
+        out = [cores[r] for r in dests]
+        Wj = T.tables["WID"][j]
+        if pos <= 2:
+            blk = T.idh[:, (pos - 1) * Wj:pos * Wj]
+            g.vector.memset(T.half[:, 0:Wj], -0.5).then_inc(sem.on, 1)
+            g.wait_ge(sem.on, 1)
+            g.affine_select(blk, T.half[:, 0:Wj], [[-1, Wj]], AluOpType.is_equal, 0.0, 0, 1).then_inc(sem.idn, 1)
+            g.wait_ge(sem.idn, 1)
+            n = _send(g, T, topo, core, [home], blk, blk, sem.ci, out)
+        else:
+            blk = T.zz[:, (pos - 3) * KW:(pos - 2) * KW]
+            g.vector.memset(blk, 0.0).then_inc(sem.on, 1)
+            g.wait_ge(sem.on, 1)
+            n = _send(g, T, topo, core, [home], blk, blk, sem.cz, out)
+        landed = bin(topo.mask(home, core)).count("1")
         g.wait_ge(sem.hk, landed)
-        n = _send(g, T, topo, core, [cores[r] for r in dests], T.kd[:], kslot(j), sem["ka%d" % j])
+        n += _send(g, T, topo, core, out, T.kd[:], kslot(j), sem["ka%d" % j])
         g.wait_ge(sem.hv, landed)
-        n += _send(g, T, topo, core, [cores[r] for r in dests], T.vd[:], vslot(j), sem["va%d" % j])
+        n += _send(g, T, topo, core, out, T.vd[:], vslot(j), sem["va%d" % j])
         g.wait_ge(sem.sent, n)
         return
 
@@ -181,27 +219,22 @@ def rank_program(g, core, T, topo):
     sent += _send(g, T, topo, core, carriers, T.vd[:], T.vd[:], sem.hv)
     sent += _send(g, T, topo, core, direct, T.vd[:], vslot(rank), sem["va%d" % rank])
 
-    ve.memset(T.half[:], -0.5).then_inc(sem.on, 1)
-    ve.memset(T.zz[:], 0.0).then_inc(sem.on, 1)
+    got = {1: 0, 3: 0}
+    for pos, (x, ds) in enumerate(carry[rank]):
+        if pos > 0:
+            got[1 if pos <= 2 else 3] += bin(_mask(topo, x, [core] + [cores[r] for r in ds])).count("1")
+
     ps = [T["ps%d" % b] for b in range(NBANK)]
     pa = [T.pa0, T.pa1, T.py]
     NA = len(pa)
     for b in range(NBANK):
         ve.memset(ps[b][:, W:2 * W], 0.0).then_inc(sem.mz, 1)
-    g.wait_ge(sem.on, 2)
-    for h in range(2):
-        g.affine_select(T.idh[0:W, h * W:(h + 1) * W], T.half[0:W, h * W:(h + 1) * W], [[-1, W]], AluOpType.is_equal, 0.0,
-                        0, 1).then_inc(sem.idn, 1)
 
     arrive = {}
     for j in range(N):
         for x, ds in carry[j]:
-            for r in ds:
-                if r == rank:
-                    m = topo.mask(x, core)
-                    for r2 in ds:
-                        m &= topo.mask(x, cores[r2])
-                    arrive[j] = bin(m).count("1")
+            if rank in ds:
+                arrive[j] = bin(_mask(topo, x, [cores[r2] for r2 in ds])).count("1")
     q = T.qs[:, 0:W]
 
     def scores(i, j):
@@ -210,7 +243,6 @@ def rank_program(g, core, T, topo):
     te.wait_ge(sem.lds, 32)
     te.wait_ge(sem.mz, NBANK)
     te.matmul(pa[(N - 1) % NA][0:W, KW:2 * KW], q, kslot(rank), True, True).then_inc(sem.fl, 1)
-    ve.wait_ge(sem.on, 2)
     ve.wait_ge(sem.fl, 1)
     for i, j in enumerate(order[rank]):
         if j != rank:
@@ -227,6 +259,7 @@ def rank_program(g, core, T, topo):
         if i == N - 2:
             ve.wait_ge(sem.mx, N - 1)
             ve.tensor_reduce(T.mm[0:W, 0:1], T.mc[0:W, 0:N - 1], AxisListType.X, AluOpType.max).then_inc(sem.tr, 1)
+            ve.wait_ge(sem.cz, got[3])
         if i == N - 1:
             ve.wait_ge(sem.tr, 1)
             ve.tensor_tensor_scan(T.mb[0:W, 0:2 * KW], bank[0:W, 0:2 * KW], T.zz[0:W, 0:2 * KW], T.mm[0:W, 0:1],
@@ -235,17 +268,23 @@ def rank_program(g, core, T, topo):
         if i >= N - LATE:
             scores(i, j)
 
+    te.wait_ge(sem.ci, got[1])
     te.wait_ge(sem.dr, 1)
-    te.wait_ge(sem.idn, 2)
     for b in range(NBANK):
         te.matmul(ps[b][:, 0:2 * W], T.mb[0:W, KW:2 * KW], T.idh[0:W, 0:2 * W], False, True).then_inc(sem.sb, 1)
-        ve.wait_ge(sem.sb, b + 1)
-        ve.tensor_scalar(T.p[:, 2 * b * W:2 * (b + 1) * W], ps[b][:, 0:2 * W], 0.0, None,
-                         AluOpType.max).then_inc(sem.rl, 1)
+        if b % 2 == 0:
+            ve.wait_ge(sem.sb, b + 1)
+            ve.tensor_scalar(T.p[:, 2 * b * W:2 * (b + 1) * W], ps[b][:, 0:2 * W], 0.0, None,
+                             AluOpType.max).then_inc(sem.rl, 1)
+        else:
+            sc.wait_ge(sem.sb, b + 1)
+            sc.activation(T.p[:, 2 * b * W:2 * (b + 1) * W], ps[b][:, 0:2 * W],
+                          ActivationFunctionType.Relu).then_inc(sem.rs, 1)
 
     for i, j in enumerate(order[rank]):
         if i % 2 == 0:
-            te.wait_ge(sem.rl, i // 2 + 1)
+            b = i // 2
+            te.wait_ge(sem.rl if b % 2 == 0 else sem.rs, b // 2 + 1)
         if j == rank:
             te.wait_ge(sem.lsv, 16)
         else:

from concourse.bass import DstId, RemoteDMATransfer
from concourse.mybir import AluOpType, AxisListType, ActivationFunctionType

NCORES = 256
N = 10
KW = 128
NDIRECT = 3
NBANK = N // 2
LATE = 5
WSHORT = 32
STARTS = 12

SCRATCH = {
    "kd": ("dram", [128, KW], "bfloat16"),
    "vd": ("dram", [128, KW], "bfloat16"),
    "kk": ("sbuf", [128, N * KW], "bfloat16"),
    "vv": ("sbuf", [128, N * KW], "bfloat16"),
    "qs": ("sbuf", [128, 64], "bfloat16"),
    "half": ("sbuf", [128, KW], "bfloat16"),
    "idh": ("sbuf", [128, KW], "bfloat16"),
    "zz": ("sbuf", [128, 2 * KW], "float32"),
    "mb": ("sbuf", [128, 2 * KW], "bfloat16"),
    "mc": ("sbuf", [128, 16], "float32"),
    "mm": ("sbuf", [128, 4], "float32"),
    "p": ("sbuf", [128, N * 64], "bfloat16"),
    "ysb": ("sbuf", [128, 64], "bfloat16"),
    "pa0": ("psum", [128, 512], "float32"),
    "pa1": ("psum", [128, 512], "float32"),
    "ps0": ("psum", [128, 512], "float32"),
    "ps1": ("psum", [128, 512], "float32"),
    "ps2": ("psum", [128, 512], "float32"),
    "ps3": ("psum", [128, 512], "float32"),
    "ps4": ("psum", [128, 512], "float32"),
    "py": ("psum", [128, 512], "float32"),
}
SEMAPHORES = (["ldk", "ldv", "lds", "lsv", "hk", "hv", "sent", "on", "mz", "idn", "ci", "cz", "fl", "st", "mx", "tr", "dr",
               "sb", "rl", "rs", "yd", "yc", "stored"] + ["ka%d" % j for j in range(N)] + ["va%d" % j for j in range(N)])

_CACHE = {}


def _combos(items, k):
    if k == 0:
        return [[]]
    out = []
    for i in range(len(items) - k + 1):
        for rest in _combos(items[i + 1:], k - 1):
            out.append([items[i]] + rest)
    return out


def _plan(T, topo):
    if "plan" in _CACHE:
        return _CACHE["plan"]
    cores = list(T.cores)
    wid = list(T.tables["WID"])

    def where(c):
        return (topo.host(c), topo.chip(c))

    mate_of = {}

    def mate_chip(c):
        if where(c) not in mate_of:
            mate_of[where(c)] = [where(m) for m in range(NCORES) if topo.mates(c, m)][0]
        return mate_of[where(c)]

    def links(x, d):
        if where(x) == where(d):
            return []
        die = topo.die(x)
        if topo.same_plane(x, d):
            return [("out", where(x), die), ("in", where(d), die)]
        way = [("mate", where(x), die)]
        if not topo.mates(x, d):
            way += [("out", mate_chip(x), die), ("in", where(d), die)]
        return way

    def wide_first(rs):
        return sorted(rs, key=lambda r: (-wid[r], r))

    def over(r):
        return max(wid[r] - WSHORT, 0)

    options = {}
    for j in range(N):
        c0 = cores[j]
        others = [r for r in range(N) if r != j]
        same = [r for r in others if topo.may_write(c0, cores[r])]
        owners = [c for c in range(NCORES) if where(c) == where(c0) and c != c0
                  and all(topo.may_write(c, cores[r]) for r in others)]
        far = [c for c in owners if topo.die(c) != topo.die(c0)]
        near = [c for c in owners if topo.die(c) == topo.die(c0)]
        options[j] = []
        for direct in _combos(same, NDIRECT):
            rest = [r for r in others if r not in direct]
            for f in _combos(rest, 4):
                nr = wide_first([r for r in rest if r not in f])
                d = wide_first(direct)
                fs = wide_first(f)
                opt = [(c0, d), (far[0], [fs[0], fs[2]]), (far[1], [fs[1], fs[3]]), (near[0], nr[:1]), (near[1], nr[1:])]
                use = []
                for x, ds in opt:
                    for r in ds:
                        use += links(x, cores[r])
                late = 100 * (over(fs[2]) + over(fs[3])) + 10 * over(d[-1])
                options[j].append((opt, use, late))

    def cost(pick):
        load = {}
        for j in range(N):
            for l in options[j][pick[j]][1]:
                load[l] = load.get(l, 0) + 1
        return sum(v ** 3 for v in load.values()) + sum(options[j][pick[j]][2] for j in range(N))

    found = None
    for s in range(STARTS):
        pick = [(s * 7 + j * 3) % len(options[j]) if s else 0 for j in range(N)]
        best = cost(pick)
        changed = True
        while changed:
            changed = False
            for j in range(N):
                for o in range(len(options[j])):
                    trial = pick[:j] + [o] + pick[j + 1:]
                    c = cost(trial)
                    if c < best:
                        best, pick, changed = c, trial, True
        if found is None or best < found[0]:
            found = (best, pick)
    pick = found[1]

    carry = {j: options[j][pick[j]][0] for j in range(N)}
    helper = {}
    due = {r: [(-1.0, r)] for r in range(N)}
    for j in range(N):
        for pos, (x, ds) in enumerate(carry[j]):
            if pos > 0:
                helper[x] = (j, ds, pos)
            for n, r in enumerate(ds):
                due[r].append(((n if pos == 0 else 2.0 + n + 0.25 * pos), j))
    order = {r: [j for _, j in sorted(due[r])] for r in range(N)}
    _CACHE["plan"] = (carry, helper, order)
    return _CACHE["plan"]


def _mask(topo, core, reach):
    mask = topo.mask(core, reach[0])
    for d in reach:
        mask &= topo.mask(core, d)
    return mask


def _send(g, T, topo, core, dst_cores, src, dst, rsem, reach=None):
    mask = _mask(topo, core, list(dst_cores) + list(reach or []))
    ids = []
    for d in dst_cores:
        rid, pid = topo.addr(d, core)
        ids.append(DstId(rid=rid, pnc=pid))
    g.remote_dma_fused([RemoteDMATransfer(dst_ids=ids, dma_engine_mask=mask, remote_sem=rsem, srcs=[src],
                                          dsts=[dst] * len(ids), alu_op=0)], local_sem=T.sem.sent)
    return bin(mask).count("1")


def rank_program(g, core, T, topo):
    carry, helper, order = _plan(T, topo)
    cores = list(T.cores)
    sem = T.sem
    rank = T.rank_of(core)

    def kslot(j):
        return T.kk[:, j * KW:(j + 1) * KW]

    def vslot(j):
        return T.vv[:, j * KW:(j + 1) * KW]

    if rank is None:
        if core not in helper:
            return
        j, dests, pos = helper[core]
        home = cores[j]
        out = [cores[r] for r in dests]
        Wj = T.tables["WID"][j]
        if pos <= 2:
            blk = T.idh[:, (pos - 1) * Wj:pos * Wj]
            g.vector.memset(T.half[:, 0:Wj], -0.5).then_inc(sem.on, 1)
            g.wait_ge(sem.on, 1)
            g.affine_select(blk, T.half[:, 0:Wj], [[-1, Wj]], AluOpType.is_equal, 0.0, 0, 1).then_inc(sem.idn, 1)
            g.wait_ge(sem.idn, 1)
            n = _send(g, T, topo, core, [home], blk, blk, sem.ci, out)
        else:
            blk = T.zz[:, (pos - 3) * KW:(pos - 2) * KW]
            g.vector.memset(blk, 0.0).then_inc(sem.on, 1)
            g.wait_ge(sem.on, 1)
            n = _send(g, T, topo, core, [home], blk, blk, sem.cz, out)
        landed = bin(topo.mask(home, core)).count("1")
        g.wait_ge(sem.hk, landed)
        n += _send(g, T, topo, core, out, T.kd[:], kslot(j), sem["ka%d" % j])
        g.wait_ge(sem.hv, landed)
        n += _send(g, T, topo, core, out, T.vd[:], vslot(j), sem["va%d" % j])
        g.wait_ge(sem.sent, n)
        return

    W = T.tables["WID"][rank]
    te, ve, sy, sc = g.tensor, g.vector, g.sync, g.scalar

    sy.dma_start(T.kd[:], T.k[:]).then_inc(sem.ldk, 16)
    sc.dma_start(T.vd[:], T.v[:]).then_inc(sem.ldv, 16)
    sy.dma_start(kslot(rank), T.k[:]).then_inc(sem.lds, 16)
    sc.dma_start(T.qs[:], T.q[:]).then_inc(sem.lds, 16)
    sc.dma_start(vslot(rank), T.v[:]).then_inc(sem.lsv, 16)

    carriers = [x for x, _ in carry[rank][1:]]
    direct = [cores[r] for r in carry[rank][0][1]]
    g.wait_ge(sem.ldk, 16)
    sent = _send(g, T, topo, core, carriers, T.kd[:], T.kd[:], sem.hk)
    sent += _send(g, T, topo, core, direct, T.kd[:], kslot(rank), sem["ka%d" % rank])
    g.wait_ge(sem.ldv, 16)
    sent += _send(g, T, topo, core, carriers, T.vd[:], T.vd[:], sem.hv)
    sent += _send(g, T, topo, core, direct, T.vd[:], vslot(rank), sem["va%d" % rank])

    got = {1: 0, 3: 0}
    for pos, (x, ds) in enumerate(carry[rank]):
        if pos > 0:
            got[1 if pos <= 2 else 3] += bin(_mask(topo, x, [core] + [cores[r] for r in ds])).count("1")

    ps = [T["ps%d" % b] for b in range(NBANK)]
    pa = [T.pa0, T.pa1, T.py]
    NA = len(pa)
    for b in range(NBANK):
        ve.memset(ps[b][:, W:2 * W], 0.0).then_inc(sem.mz, 1)

    arrive = {}
    for j in range(N):
        for x, ds in carry[j]:
            if rank in ds:
                arrive[j] = bin(_mask(topo, x, [cores[r2] for r2 in ds])).count("1")
    q = T.qs[:, 0:W]

    def scores(i, j):
        te.matmul(ps[i // 2][:, (i % 2) * W:(i % 2 + 1) * W], kslot(j), q, i % 2 == 0, False)

    te.wait_ge(sem.lds, 32)
    te.wait_ge(sem.mz, NBANK)
    te.matmul(pa[(N - 1) % NA][0:W, KW:2 * KW], q, kslot(rank), True, True).then_inc(sem.fl, 1)
    ve.wait_ge(sem.fl, 1)
    for i, j in enumerate(order[rank]):
        if j != rank:
            te.wait_ge(sem["ka%d" % j], arrive[j])
        if i >= NA:
            te.wait_ge(sem.mx, i - NA + 1)
        bank = pa[i % NA]
        te.matmul(bank[0:W, 0:KW], q, kslot(j), True, True).then_inc(sem.st, 1)
        if i < N - LATE:
            scores(i, j)
        ve.wait_ge(sem.st, i + 1)
        if i < N - 1:
            ve.tensor_reduce(T.mc[0:W, i:i + 1], bank[0:W, 0:KW], AxisListType.X, AluOpType.max).then_inc(sem.mx, 1)
        if i == N - 2:
            ve.wait_ge(sem.mx, N - 1)
            ve.tensor_reduce(T.mm[0:W, 0:1], T.mc[0:W, 0:N - 1], AxisListType.X, AluOpType.max).then_inc(sem.tr, 1)
            ve.wait_ge(sem.cz, got[3])
        if i == N - 1:
            ve.wait_ge(sem.tr, 1)
            ve.tensor_tensor_scan(T.mb[0:W, 0:2 * KW], bank[0:W, 0:2 * KW], T.zz[0:W, 0:2 * KW], T.mm[0:W, 0:1],
                                  AluOpType.max, AluOpType.add).then_inc(sem.dr, 1)
    for i, j in enumerate(order[rank]):
        if i >= N - LATE:
            scores(i, j)

    te.wait_ge(sem.ci, got[1])
    te.wait_ge(sem.dr, 1)
    for b in range(NBANK):
        te.matmul(ps[b][:, 0:2 * W], T.mb[0:W, KW:2 * KW], T.idh[0:W, 0:2 * W], False, True).then_inc(sem.sb, 1)
        if b % 2 == 0:
            ve.wait_ge(sem.sb, b + 1)
            ve.tensor_scalar(T.p[:, 2 * b * W:2 * (b + 1) * W], ps[b][:, 0:2 * W], 0.0, None,
                             AluOpType.max).then_inc(sem.rl, 1)
        else:
            sc.wait_ge(sem.sb, b + 1)
            sc.activation(T.p[:, 2 * b * W:2 * (b + 1) * W], ps[b][:, 0:2 * W],
                          ActivationFunctionType.Relu).then_inc(sem.rs, 1)

    for i, j in enumerate(order[rank]):
        if i % 2 == 0:
            b = i // 2
            te.wait_ge(sem.rl if b % 2 == 0 else sem.rs, b // 2 + 1)
        if j == rank:
            te.wait_ge(sem.lsv, 16)
        else:
            te.wait_ge(sem["va%d" % j], arrive[j])
        mm = te.matmul(T.py[:, 0:W], vslot(j), T.p[:, i * W:(i + 1) * W], i == 0, i == N - 1)
        if i == N - 1:
            mm.then_inc(sem.yd, 1)
    ve.wait_ge(sem.yd, 1)
    ve.tensor_copy(T.ysb[:, 0:W], T.py[:, 0:W]).then_inc(sem.yc, 1)
    sy.wait_ge(sem.yc, 1)
    sy.dma_start(T.y[:, 0:W], T.ysb[:, 0:W]).then_inc(sem.stored, 16)
    sy.wait_ge(sem.stored, 16)
    g.wait_ge(sem.sent, sent)
